import numpy as np, ml_dtypes
CORES = [3,1,0,2]
N = 4
def setup_inputs(rng):
    return {"x": rng.standard_normal((N, 128, 4096), dtype=np.float32).astype(ml_dtypes.bfloat16)}
def reference(x):
    g = np.concatenate(list(x), axis=1)
    return {"y": np.broadcast_to(g, (N,) + g.shape)}

import concourse.bass as bass

BLOCK = 4096
RANKS = 4
ENGINES = 16

SCRATCH = {
    "img": ("sbuf", [128, RANKS * BLOCK], "bfloat16"),
}
SEMAPHORES = ["loaded", "sent", "arrived", "stored"]


def rank_program(g, core, T, topo):
    rank = T.rank_of(core)
    if rank is None:
        return

    mine = T.img[:, rank * BLOCK:(rank + 1) * BLOCK]
    peers = [c for c in T.cores if c != core]

    g.dma_start(mine, T.x[:]).then_inc(T.sem.loaded, 16)
    g.wait_ge(T.sem.loaded, 16)

    dst_ids = []
    for p in peers:
        rid, pid, ring = topo.addr(p)
        dst_ids.append(bass.DstId(rid=rid, pnc=pid))
    g.remote_dma_fused(
        [bass.RemoteDMATransfer(
            dst_ids=dst_ids,
            dma_engine_mask=topo.mask(core, peers[0]),
            remote_sem=T.sem.arrived,
            srcs=[mine],
            dsts=[mine for p in peers],
            alu_op=0,
        )],
        local_sem=T.sem.sent,
    )

    g.wait_ge(T.sem.arrived, ENGINES * len(peers))
    g.dma_start(T.y[:], T.img[:]).then_inc(T.sem.stored, 16)
    g.wait_ge(T.sem.sent, ENGINES)
    g.wait_ge(T.sem.stored, 16)
